import numpy as np
import ml_dtypes


def mxq(x, axis, fmt="e4m3"):
    dtype, down = {"e4m3": (ml_dtypes.float8_e4m3fn, 7), "e5m2": (ml_dtypes.float8_e5m2, 14)}[fmt]
    v = np.moveaxis(np.asarray(x, np.float32).astype(ml_dtypes.bfloat16).astype(np.float64), axis, -1)
    blocks = v.reshape(v.shape[:-1] + (-1, 32))
    amax = np.abs(blocks).max(-1, keepdims=True)
    byte = np.maximum(np.where(amax > 0, np.frexp(amax)[1] - 1 + 127, 0) - down, 1)
    scale = np.exp2(byte - 127.0)
    codes = (blocks / scale).astype(np.float32).astype(dtype).astype(np.float64)
    return np.moveaxis((codes * scale).reshape(v.shape), -1, axis)


WIDE = False


def mx_kscale(k):
    if not WIDE:
        return np.ones(k)
    levels = np.array([10, -10, 5, -5, 0])
    if k % 512:
        return np.exp2(np.random.permutation(np.resize(levels, k // 32))).repeat(32)
    a = np.empty((k // 512, 16))
    for p in range(k // 512):
        a[p, :8] = np.random.permutation(np.resize(levels, 8))
        for g in range(8):
            far = levels[np.abs(levels - a[p, g]) >= 10]
            a[p, g + 8] = far[np.random.randint(len(far))]
    return np.exp2(a.ravel()).repeat(32)


def f64(x):
    return np.asarray(x).astype(np.float64)


def striped(idx):
    return np.tile(idx.reshape(-1, 16).T, (8, 1)).astype(np.uint16)


def unstriped(offs):
    return offs[:16].T.reshape(-1).astype(np.int64)


def striped8(idx):
    return np.concatenate([x.reshape(-1, 16).T for x in idx]).astype(np.uint16)


def runs(offs, k):
    lists = np.stack([offs[16 * r : 16 * r + 16].T.reshape(-1) for r in range(8)]).astype(np.int64)
    return lists[np.arange(k) % 512 // 64]


def pack_weight(w):
    k, n = w.shape
    w = f64(np.asarray(w, np.float32).astype(ml_dtypes.bfloat16)).reshape(k // 32, 32, n)
    amax = np.abs(w).max(1)
    byte = np.clip(np.where(amax > 0, np.frexp(amax)[1] - 1 + 127 - 7, 1), 1, 254)
    scaled = (w * np.exp2(127.0 - byte)[:, None, :]).reshape(k, n).astype(np.float32)
    words = np.ascontiguousarray(scaled.reshape(k // 512, 128, 4, n).transpose(0, 1, 3, 2)).astype(ml_dtypes.float8_e4m3fn).view(np.uint8)
    return words, np.ascontiguousarray(byte.astype(np.uint8).reshape(k // 512, 16, n))


def unpack_weight(words, scales):
    g, p, n, _ = words.shape
    vals = np.ascontiguousarray(words).view(ml_dtypes.float8_e4m3fn).astype(np.float64) * np.repeat(np.exp2(scales.astype(np.float64) - 127.0), 8, axis=1)[..., None]
    return vals.transpose(0, 1, 3, 2).reshape(g * 512, n)


def sigmoid(v):
    return 1.0 / (1.0 + np.exp(-np.maximum(v, -700.0)))


K, T, S, N, H = 512, 2048, 512, 512, 512


def setup_inputs():
    n = np.random.standard_normal
    s = mx_kscale(K)[:, None]
    u = mx_kscale(H)
    packed_xT = pack_weight(n((K, T)) * s)
    return {
        "x_words": packed_xT[0],
        "x_scales": packed_xT[1],
        "w1": (n((K, H)) / np.sqrt(K) / s).astype(np.float32),
        "gn": (np.random.uniform(0.5, 1.5, (H, 1)) * u[:, None]).astype(np.float32),
        "w2": (n((H, N)) / np.sqrt(H) / u[:, None]).astype(np.float32),
        "offs": striped(np.random.permutation(T)[:S]),
        "n1": striped8(np.stack([np.random.permutation(S) for _ in range(8)])),
        "n2": striped8(np.stack([np.random.permutation(S) for _ in range(8)])),
        "n3": striped8(np.stack([np.random.permutation(S) for _ in range(8)])),
        "n4": striped8(np.stack([np.random.permutation(S) for _ in range(8)])),
    }


def reference(x_words, x_scales, w1, gn, w2, offs, n1, n2, n3, n4):
    xq = unpack_weight(x_words, x_scales)[:, unstriped(offs)]
    y = mxq(f64(w1), 0, "e4m3").T @ xq
    th = np.tanh(y)
    z = f64(gn) * (th * (th[np.arange(H)[:, None], runs(n1, H)]) - (0.5 * (th[np.arange(H)[:, None], runs(n2, H)])))
    h = mxq(f64(w2), 0, "e4m3").T @ mxq(z, 0, "e4m3")
    a = h[np.arange(N)[:, None], runs(n3, N)]
    b = h[np.arange(N)[:, None], runs(n4, N)]
    return h + sigmoid(a - b) * (b - h)

@@ -1,0 +1,205 @@
+from contextlib import ExitStack
+
+import concourse.mybir as mybir
+from concourse.masks import make_identity
+
+K, T, S, H, N = 512, 2048, 512, 512, 512
+FLOPS = 2 * K * H * S + 2 * H * N * S
+
+F32 = mybir.dt.float32
+BF16 = mybir.dt.bfloat16
+I32 = mybir.dt.int32
+U32 = mybir.dt.uint32
+U16 = mybir.dt.uint16
+U8 = mybir.dt.uint8
+FP8X4 = mybir.dt.float8_e4m3fn_x4
+ALU = mybir.AluOpType
+ACT = mybir.ActivationFunctionType
+
+P = 128
+PACK = 4
+LIST_ROWS = 16
+HALF = S // 2
+Z_CHUNKS = ((0, 256), (256, 384), (384, 512))
+
+
+def tile_picked_tanmix_none_p_kernel(tc, x_words, x_scales, w1, gn, w2, offs, n1, n2, n3, n4, out):
+    nc = tc.nc
+    with ExitStack() as ctx:
+        lists = ctx.enter_context(tc.tile_pool(name="lists", bufs=1))
+        keep = ctx.enter_context(tc.tile_pool(name="keep", bufs=1))
+        psum = ctx.enter_context(tc.psum_pool(name="psum", bufs=1))
+
+        def bank(b, name):
+            return psum.tile([P, S], F32, name=name, tag=f"bank{b}")
+
+        def entries(lst, lo, hi):
+            return lst[:, lo // LIST_ROWS : hi // LIST_ROWS]
+
+        def load_list(src, name):
+            lst = lists.tile([P, S // LIST_ROWS], U16, name=name)
+            nc.sync.dma_start(lst[:], src)
+            return lst
+
+        xs_win = keep.tile([P, T], U8, name="xs_win", align_bytes=64)
+        nc.gpsimd.memset(xs_win[:].bitcast(I32), 0)
+        offs_t = load_list(offs, "offs_t")
+        for q in range(4):
+            nc.scalar.dma_start(xs_win[32 * q : 32 * q + 4, :].bitcast(I32), x_scales[0][4 * q : 4 * q + 4, :].bitcast(I32))
+        w1_raw = keep.tile([P, PACK, H], F32, name="w1_raw")
+        nc.sync.dma_start(w1_raw[:], w1.rearrange("(p j) c -> p j c", j=PACK))
+        xw_win = keep.tile([P, T], U32, name="xw_win", align_bytes=64)
+        nc.sync.dma_start(xw_win[:].bitcast(I32), x_words[0].rearrange("p n r -> p (n r)").bitcast(I32))
+        gain = keep.tile([P, PACK], F32, name="gain")
+        nc.sync.dma_start(gain[:], gn.rearrange("(p t) o -> p (t o)", t=PACK))
+        n1_t = load_list(n1, "n1_t")
+        w2_rows = w2.rearrange("(p j) c -> p j c", j=PACK)
+        w2_raw = []
+        for hf in range(2):
+            part = keep.tile([P, PACK, N // 2], F32, name=f"w2_raw{hf}")
+            nc.sync.dma_start(part[:], w2_rows[:, :, hf * (N // 2) : (hf + 1) * (N // 2)])
+            w2_raw.append(part)
+        n2_t = load_list(n2, "n2_t")
+        n4_t = load_list(n4, "n4_t")
+        n3_t = load_list(n3, "n3_t")
+
+        warm = keep.tile([P, 2], F32, name="warm")
+        nc.gpsimd.memset(warm[:], 0.0)
+        nc.scalar.activation(warm[:, 1:2], warm[:, 0:1], ACT.Tanh)
+
+        ident = keep.tile([P, P], F32, name="ident")
+        make_identity(nc, ident[:])
+        win_pos = [keep.tile([P, 2 * S], F32, name=f"win_pos{t}") for t in range(PACK)]
+        win_neg = [keep.tile([P, 2 * S], F32, name=f"win_neg{t}") for t in range(PACK)]
+        for t in range(PACK):
+            nc.vector.memset(win_pos[t][:, S:], 0.0)
+            nc.gpsimd.memset(win_neg[t][:, S:], 0.0)
+
+        xs_g = keep.tile([P, S], U8, name="xs_g", align_bytes=64)
+        nc.vector.tensor_copy(xs_g[:], xs_win[:].indirect(offs_t[:]))
+
+        def deal(copy, grouped, raw, m_lo, m_hi, c_lo):
+            n = m_hi - m_lo
+            copy(
+                grouped[:, :, m_lo:m_hi, :].rearrange("p t m j -> p m j t"),
+                raw[:, :, c_lo : c_lo + PACK * n].rearrange("p j (m t) -> p m j t", t=PACK),
+            )
+
+        w1_bf = keep.tile([P, PACK, P, PACK], BF16, name="w1_bf", align_bytes=64)
+        deal(nc.scalar.copy, w1_bf, w1_raw, 0, 64, 0)
+        deal(nc.vector.tensor_copy, w1_bf, w1_raw, 64, 128, 256)
+        w1_q = keep.tile([P, H], U32, name="w1_q", align_bytes=64)
+        w1_s = keep.tile([P, H], U8, name="w1_s", align_bytes=64)
+        nc.vector.quantize_mx(w1_q[:].bitcast(FP8X4), w1_s[:], w1_bf[:].rearrange("p t m j -> p (t m j)"))
+
+        gain_neg_half = keep.tile([P, PACK], F32, name="gain_neg_half")
+        nc.gpsimd.tensor_scalar(gain_neg_half[:], gain[:], -0.5, 0.0, ALU.mult, ALU.add)
+
+        xw_g = keep.tile([P, S], U32, name="xw_g", align_bytes=64)
+        for hf in range(2):
+            nc.vector.tensor_copy(xw_g[:, hf * HALF : (hf + 1) * HALF], xw_win[:].indirect(entries(offs_t, hf * HALF, (hf + 1) * HALF)))
+
+        def product(acc, wq, ws, t, xq, xs, lo, hi):
+            nc.tensor.matmul_mx(
+                acc[:, lo:hi],
+                lhsT=wq[:, t * P : (t + 1) * P].bitcast(FP8X4),
+                lhsT_scale=ws[:, t * P : (t + 1) * P],
+                rhs=xq[:, lo:hi].bitcast(FP8X4),
+                rhs_scale=xs[:, lo:hi],
+                start=True,
+                stop=True,
+            )
+
+        w2_bf = keep.tile([P, PACK, P, PACK], BF16, name="w2_bf", align_bytes=64)
+        deal(nc.vector.tensor_copy, w2_bf, w2_raw[0], 0, 64, 0)
+
+        gth = [keep.tile([P, S], F32, name=f"gth{t}") for t in range(PACK)]
+        half_gth = [keep.tile([P, S], F32, name=f"half_gth{t}") for t in range(PACK)]
+        prod = [keep.tile([P, S], F32, name=f"prod{t}") for t in range(PACK)]
+        for t in range(PACK):
+            th = win_pos[t]
+            if t == 0:
+                for hf in range(2):
+                    lo, hi = hf * HALF, (hf + 1) * HALF
+                    y = bank(hf, f"y0_{hf}")
+                    product(y, w1_q, w1_s, t, xw_g, xs_g, lo, hi)
+                    nc.scalar.activation(th[:, lo:hi], y[:, lo:hi], ACT.Tanh)
+                    nc.vector.tensor_scalar(gth[t][:, lo:hi], th[:, lo:hi], gain[:, t : t + 1], None, ALU.mult)
+            else:
+                y = bank(t + 1, f"y{t}")
+                product(y, w1_q, w1_s, t, xw_g, xs_g, 0, S)
+                nc.scalar.activation(th[:, :S], y[:], ACT.Tanh)
+                nc.scalar.activation(gth[t][:], th[:, :S], ACT.Copy, scale=gain[:, t : t + 1])
+            nc.vector.tensor_tensor(prod[t][:], th[:].indirect(n1_t[:]), gth[t][:], ALU.mult)
+        for t in range(PACK):
+            nc.scalar.activation(half_gth[t][:], win_pos[t][:, :S], ACT.Copy, scale=gain_neg_half[:, t : t + 1])
+        deal(nc.scalar.copy, w2_bf, w2_raw[1], 64, 128, 0)
+
+        w2_q = keep.tile([P, N], U32, name="w2_q", align_bytes=64)
+        w2_s = keep.tile([P, N], U8, name="w2_s", align_bytes=64)
+        z_q = keep.tile([P, S], U32, name="z_q", align_bytes=64)
+        z_s = keep.tile([P, S], U8, name="z_s", align_bytes=64)
+        z_bf = []
+        last = len(Z_CHUNKS) - 1
+
+        def quantise_z(c):
+            lo, hi = Z_CHUNKS[c]
+            nc.vector.quantize_mx(z_q[:, lo:hi].bitcast(FP8X4), z_s[:, lo:hi], z_bf[c][:].rearrange("p s t -> p (s t)"))
+
+        for c, (lo, hi) in enumerate(Z_CHUNKS):
+            z = keep.tile([P, PACK, hi - lo], F32, name=f"z{c}")
+            for t in range(PACK):
+                nc.vector.tensor_tensor(z[:, t, :], half_gth[t][:].indirect(entries(n2_t, lo, hi)), prod[t][:, lo:hi], ALU.add)
+            zb = keep.tile([P, hi - lo, PACK], BF16, name=f"z_bf{c}", align_bytes=64)
+            z_bf.append(zb)
+            if c == 1:
+                nc.vector.quantize_mx(w2_q[:].bitcast(FP8X4), w2_s[:], w2_bf[:].rearrange("p t m j -> p (t m j)"))
+            if c > 0:
+                quantise_z(c - 1)
+            copy = nc.vector.tensor_copy if c == last else nc.scalar.copy
+            copy(zb[:].rearrange("p (s i) t -> p s t i", i=PACK), z[:].rearrange("p t (s i) -> p s t i", i=PACK))
+        quantise_z(last)
+
+        split = Z_CHUNKS[last][0]
+        e = [keep.tile([P, S], F32, name=f"e{t}") for t in range(PACK)]
+        f = [keep.tile([P, S], F32, name=f"f{t}") for t in range(PACK)]
+        tau = []
+        d_bank = (5, 7, 5, 7)
+        tau_bank = (6, 0, 1, 2)
+        for t in range(PACK):
+            if t == 0:
+                h_a = bank(0, "h0_a")
+                for lo, hi in Z_CHUNKS[:last]:
+                    product(h_a, w2_q, w2_s, t, z_q, z_s, lo, hi)
+                h_b = bank(1, "h0_b")
+                product(h_b, w2_q, w2_s, t, z_q, z_s, split, S)
+                pieces = ((h_a, 0, split), (h_b, split, S))
+            else:
+                h = bank(t + 1, f"h{t}")
+                product(h, w2_q, w2_s, t, z_q, z_s, 0, S)
+                pieces = ((h, 0, S),)
+            for acc, lo, hi in pieces:
+                nc.scalar.copy(win_pos[t][:, lo:hi], acc[:, lo:hi])
+                nc.scalar.activation(win_neg[t][:, lo:hi], acc[:, lo:hi], ACT.Copy, scale=-1.0)
+            nc.vector.tensor_tensor(e[t][:], win_pos[t][:].indirect(n4_t[:]), win_neg[t][:, :S], ALU.add)
+            nc.vector.tensor_tensor(f[t][:], win_neg[t][:].indirect(n3_t[:]), win_pos[t][:, :S], ALU.add)
+        for t in range(PACK):
+            d_t = bank(d_bank[t], f"d{t}")
+            for b in range(S // P):
+                cols = slice(b * P, (b + 1) * P)
+                nc.tensor.matmul(d_t[:, cols], e[t][:, cols], ident[:], start=True, stop=False, is_transpose=True)
+                nc.tensor.matmul(d_t[:, cols], f[t][:, cols], ident[:], start=False, stop=True, is_transpose=True)
+            tau_t = keep.tile([P, S], F32, name=f"tau_t{t}")
+            nc.scalar.activation(tau_t[:], d_t[:], ACT.Tanh, scale=-0.5)
+            back = bank(tau_bank[t], f"tau{t}")
+            for b in range(S // P):
+                cols = slice(b * P, (b + 1) * P)
+                nc.tensor.transpose(back[:, cols], tau_t[:, cols], ident[:])
+            tau.append(back)
+        out_rows = out.rearrange("(p t) s -> p t s", t=PACK)
+        for t in range(PACK):
+            step = keep.tile([P, S], F32, name=f"step{t}")
+            nc.vector.scalar_tensor_tensor(step[:], tau[t][:], 1.0, e[t][:], ALU.add, ALU.mult)
+            res = keep.tile([P, S], F32, name=f"res{t}")
+            nc.vector.scalar_tensor_tensor(res[:], step[:], 0.5, win_pos[t][:, :S], ALU.mult, ALU.add)
+            nc.sync.dma_start(out_rows[:, t, :], res[:])

@@ -41,18 +41,18 @@ def tile_picked_tanmix_none_p_kernel(tc, x_words, x_scales, w1, gn, w2, offs, n1
             nc.sync.dma_start(lst[:], src)
             return lst
 
-        xs_win = keep.tile([P, T], U8, name="xs_win", align_bytes=64)
-        nc.gpsimd.memset(xs_win[:].bitcast(I32), 0)
-        offs_t = load_list(offs, "offs_t")
-        for q in range(4):
-            nc.scalar.dma_start(xs_win[32 * q : 32 * q + 4, :].bitcast(I32), x_scales[0][4 * q : 4 * q + 4, :].bitcast(I32))
+        xs_win = keep.tile([P, T], U8, name="xs_win", tag="xs_win", align_bytes=64)
+        nc.vector.memset(xs_win[:].bitcast(I32), 0)
         w1_raw = keep.tile([P, PACK, H], F32, name="w1_raw")
         nc.sync.dma_start(w1_raw[:], w1.rearrange("(p j) c -> p j c", j=PACK))
+        offs_t = load_list(offs, "offs_t")
+        n1_t = load_list(n1, "n1_t")
+        for q in range(4):
+            nc.sync.dma_start(xs_win[32 * q : 32 * q + 4, :].bitcast(I32), x_scales[0][4 * q : 4 * q + 4, :].bitcast(I32))
         xw_win = keep.tile([P, T], U32, name="xw_win", align_bytes=64)
         nc.sync.dma_start(xw_win[:].bitcast(I32), x_words[0].rearrange("p n r -> p (n r)").bitcast(I32))
         gain = keep.tile([P, PACK], F32, name="gain")
         nc.sync.dma_start(gain[:], gn.rearrange("(p t) o -> p (t o)", t=PACK))
-        n1_t = load_list(n1, "n1_t")
         w2_rows = w2.rearrange("(p j) c -> p j c", j=PACK)
         w2_raw = []
         for hf in range(2):
@@ -65,7 +65,7 @@ def tile_picked_tanmix_none_p_kernel(tc, x_words, x_scales, w1, gn, w2, offs, n1
 
         warm = keep.tile([P, 2], F32, name="warm")
         nc.gpsimd.memset(warm[:], 0.0)
-        nc.scalar.activation(warm[:, 1:2], warm[:, 0:1], ACT.Tanh)
+        nc.scalar.activation(warm[:, 1:2], warm[:, 0:1], ACT.Sigmoid)
 
         ident = keep.tile([P, P], F32, name="ident")
         make_identity(nc, ident[:])
@@ -75,8 +75,6 @@ def tile_picked_tanmix_none_p_kernel(tc, x_words, x_scales, w1, gn, w2, offs, n1
             nc.vector.memset(win_pos[t][:, S:], 0.0)
             nc.gpsimd.memset(win_neg[t][:, S:], 0.0)
 
-        xs_g = keep.tile([P, S], U8, name="xs_g", align_bytes=64)
-        nc.vector.tensor_copy(xs_g[:], xs_win[:].indirect(offs_t[:]))
 
         def deal(copy, grouped, raw, m_lo, m_hi, c_lo):
             n = m_hi - m_lo
@@ -88,24 +86,26 @@ def tile_picked_tanmix_none_p_kernel(tc, x_words, x_scales, w1, gn, w2, offs, n1
         w1_bf = keep.tile([P, PACK, P, PACK], BF16, name="w1_bf", align_bytes=64)
         deal(nc.scalar.copy, w1_bf, w1_raw, 0, 64, 0)
         deal(nc.vector.tensor_copy, w1_bf, w1_raw, 64, 128, 256)
-        w1_q = keep.tile([P, H], U32, name="w1_q", align_bytes=64)
+        xs_g = keep.tile([P, S], U8, name="xs_g", align_bytes=64)
+        nc.vector.tensor_copy(xs_g[:], xs_win[:].indirect(offs_t[:]))
+        w1_q = keep.tile([P, H], U32, name="w1_q", tag="xs_win", align_bytes=64)
         w1_s = keep.tile([P, H], U8, name="w1_s", align_bytes=64)
         nc.vector.quantize_mx(w1_q[:].bitcast(FP8X4), w1_s[:], w1_bf[:].rearrange("p t m j -> p (t m j)"))
 
         gain_neg_half = keep.tile([P, PACK], F32, name="gain_neg_half")
         nc.gpsimd.tensor_scalar(gain_neg_half[:], gain[:], -0.5, 0.0, ALU.mult, ALU.add)
 
-        xw_g = keep.tile([P, S], U32, name="xw_g", align_bytes=64)
+        xw_g = [keep.tile([P, HALF], U32, name=f"xw_g{hf}", align_bytes=64) for hf in range(2)]
         for hf in range(2):
-            nc.vector.tensor_copy(xw_g[:, hf * HALF : (hf + 1) * HALF], xw_win[:].indirect(entries(offs_t, hf * HALF, (hf + 1) * HALF)))
+            nc.vector.tensor_copy(xw_g[hf][:], xw_win[:].indirect(entries(offs_t, hf * HALF, (hf + 1) * HALF)))
 
-        def product(acc, wq, ws, t, xq, xs, lo, hi):
+        def product(acc, wq, ws, xq, xs):
             nc.tensor.matmul_mx(
-                acc[:, lo:hi],
-                lhsT=wq[:, t * P : (t + 1) * P].bitcast(FP8X4),
-                lhsT_scale=ws[:, t * P : (t + 1) * P],
-                rhs=xq[:, lo:hi].bitcast(FP8X4),
-                rhs_scale=xs[:, lo:hi],
+                acc,
+                lhsT=wq.bitcast(FP8X4),
+                lhsT_scale=ws,
+                rhs=xq.bitcast(FP8X4),
+                rhs_scale=xs,
                 start=True,
                 stop=True,
             )
@@ -114,7 +114,7 @@ def tile_picked_tanmix_none_p_kernel(tc, x_words, x_scales, w1, gn, w2, offs, n1
         deal(nc.vector.tensor_copy, w2_bf, w2_raw[0], 0, 64, 0)
 
         gth = [keep.tile([P, S], F32, name=f"gth{t}") for t in range(PACK)]
-        half_gth = [keep.tile([P, S], F32, name=f"half_gth{t}") for t in range(PACK)]
+        half_gth = win_neg
         prod = [keep.tile([P, S], F32, name=f"prod{t}") for t in range(PACK)]
         for t in range(PACK):
             th = win_pos[t]
@@ -122,84 +122,132 @@ def tile_picked_tanmix_none_p_kernel(tc, x_words, x_scales, w1, gn, w2, offs, n1
                 for hf in range(2):
                     lo, hi = hf * HALF, (hf + 1) * HALF
                     y = bank(hf, f"y0_{hf}")
-                    product(y, w1_q, w1_s, t, xw_g, xs_g, lo, hi)
+                    product(y[:, lo:hi], w1_q[:, t * P : (t + 1) * P], w1_s[:, t * P : (t + 1) * P], xw_g[hf][:], xs_g[:, lo:hi])
                     nc.scalar.activation(th[:, lo:hi], y[:, lo:hi], ACT.Tanh)
                     nc.vector.tensor_scalar(gth[t][:, lo:hi], th[:, lo:hi], gain[:, t : t + 1], None, ALU.mult)
             else:
                 y = bank(t + 1, f"y{t}")
-                product(y, w1_q, w1_s, t, xw_g, xs_g, 0, S)
+                for hf in range(2):
+                    lo, hi = hf * HALF, (hf + 1) * HALF
+                    product(y[:, lo:hi], w1_q[:, t * P : (t + 1) * P], w1_s[:, t * P : (t + 1) * P], xw_g[hf][:], xs_g[:, lo:hi])
                 nc.scalar.activation(th[:, :S], y[:], ACT.Tanh)
                 nc.scalar.activation(gth[t][:], th[:, :S], ACT.Copy, scale=gain[:, t : t + 1])
             nc.vector.tensor_tensor(prod[t][:], th[:].indirect(n1_t[:]), gth[t][:], ALU.mult)
         for t in range(PACK):
-            nc.scalar.activation(half_gth[t][:], win_pos[t][:, :S], ACT.Copy, scale=gain_neg_half[:, t : t + 1])
+            nc.scalar.activation(half_gth[t][:, :S], win_pos[t][:, :S], ACT.Copy, scale=gain_neg_half[:, t : t + 1])
         deal(nc.scalar.copy, w2_bf, w2_raw[1], 64, 128, 0)
 
-        w2_q = keep.tile([P, N], U32, name="w2_q", align_bytes=64)
-        w2_s = keep.tile([P, N], U8, name="w2_s", align_bytes=64)
-        z_q = keep.tile([P, S], U32, name="z_q", align_bytes=64)
-        z_s = keep.tile([P, S], U8, name="z_s", align_bytes=64)
-        z_bf = []
-        last = len(Z_CHUNKS) - 1
+        w2_q0 = keep.tile([P, P], U32, name="w2_q0", align_bytes=64)
+        w2_s_all = keep.tile([P, N], U8, name="w2_s_all", align_bytes=64)
+        w2_flat = w2_bf[:].rearrange("p t m j -> p (t m j)")
+        z_q = [keep.tile([P, hi - lo], U32, name=f"z_q{c}", align_bytes=64) for c, (lo, hi) in enumerate(Z_CHUNKS)]
+        z_s = [keep.tile([P, hi - lo], U8, name=f"z_s{c}", align_bytes=64) for c, (lo, hi) in enumerate(Z_CHUNKS)]
+        last_tile = PACK - 1
+        z_bf = [keep.tile([P, hi - lo, PACK], BF16, name=f"z_bf{c}", tag=f"z_bf{c}", align_bytes=64) for c, (lo, hi) in enumerate(Z_CHUNKS)]
+        z_all = keep.tile([P, PACK, S], F32, name="z_all")
+        for t in range(PACK):
+            for lo, hi in ((0, S),) if t < last_tile else ((0, HALF), (HALF, S)):
+                nc.vector.tensor_tensor(z_all[:, t, lo:hi], half_gth[t][:].indirect(entries(n2_t, lo, hi)), prod[t][:, lo:hi], ALU.add)
+        nc.vector.quantize_mx(w2_q0[:].bitcast(FP8X4), w2_s_all[:, :P], w2_flat[:, : PACK * P])
+
+        def interleave(c, copy):
+            lo, hi = Z_CHUNKS[c]
+            copy(z_bf[c][:].rearrange("p (s i) t -> p s t i", i=PACK), z_all[:, :, lo:hi].rearrange("p t (s i) -> p s t i", i=PACK))
 
         def quantise_z(c):
-            lo, hi = Z_CHUNKS[c]
-            nc.vector.quantize_mx(z_q[:, lo:hi].bitcast(FP8X4), z_s[:, lo:hi], z_bf[c][:].rearrange("p s t -> p (s t)"))
+            nc.vector.quantize_mx(z_q[c][:].bitcast(FP8X4), z_s[c][:], z_bf[c][:].rearrange("p s t -> p (s t)"))
 
-        for c, (lo, hi) in enumerate(Z_CHUNKS):
-            z = keep.tile([P, PACK, hi - lo], F32, name=f"z{c}")
-            for t in range(PACK):
-                nc.vector.tensor_tensor(z[:, t, :], half_gth[t][:].indirect(entries(n2_t, lo, hi)), prod[t][:, lo:hi], ALU.add)
-            zb = keep.tile([P, hi - lo, PACK], BF16, name=f"z_bf{c}", align_bytes=64)
-            z_bf.append(zb)
-            if c == 1:
-                nc.vector.quantize_mx(w2_q[:].bitcast(FP8X4), w2_s[:], w2_bf[:].rearrange("p t m j -> p (t m j)"))
-            if c > 0:
-                quantise_z(c - 1)
-            copy = nc.vector.tensor_copy if c == last else nc.scalar.copy
-            copy(zb[:].rearrange("p (s i) t -> p s t i", i=PACK), z[:].rearrange("p t (s i) -> p s t i", i=PACK))
-        quantise_z(last)
+        interleave(0, nc.scalar.copy)
+        interleave(1, nc.vector.tensor_copy)
+        quantise_z(0)
+        interleave(2, nc.vector.tensor_copy)
+        quantise_z(1)
+        quantise_z(2)
+        w2_q_rest = keep.tile([P, 3 * P], U32, name="w2_q_rest", tag="z_bf2", align_bytes=64)
+        nc.vector.quantize_mx(w2_q_rest[:, :P].bitcast(FP8X4), w2_s_all[:, P : 2 * P], w2_flat[:, PACK * P : 2 * PACK * P])
+        nc.vector.quantize_mx(w2_q_rest[:, P:].bitcast(FP8X4), w2_s_all[:, 2 * P :], w2_flat[:, 2 * PACK * P :])
+        w2_q = [w2_q0[:]] + [w2_q_rest[:, u * P : (u + 1) * P] for u in range(3)]
+        w2_s = [w2_s_all[:, t * P : (t + 1) * P] for t in range(PACK)]
 
-        split = Z_CHUNKS[last][0]
-        e = [keep.tile([P, S], F32, name=f"e{t}") for t in range(PACK)]
-        f = [keep.tile([P, S], F32, name=f"f{t}") for t in range(PACK)]
-        tau = []
-        d_bank = (5, 7, 5, 7)
-        tau_bank = (6, 0, 1, 2)
-        for t in range(PACK):
+        out_rows = out.rearrange("(p t) s -> p t s", t=PACK)
+        blocks = [slice(u * P, (u + 1) * P) for u in range(S // P)]
+        res = [keep.tile([P, S], F32, name=f"res{t}") for t in range(PACK)]
+        h_first_banks = (0, 1, 5)
+        gate_bank = (0, 1, 5, 2)
+        h_banks, e, f, gate = {}, {}, {}, {}
+
+        def spans(t):
+            return ((0, S),) if t < last_tile else ((0, HALF), (HALF, S))
+
+        def second_product(t):
             if t == 0:
-                h_a = bank(0, "h0_a")
-                for lo, hi in Z_CHUNKS[:last]:
-                    product(h_a, w2_q, w2_s, t, z_q, z_s, lo, hi)
-                h_b = bank(1, "h0_b")
-                product(h_b, w2_q, w2_s, t, z_q, z_s, split, S)
-                pieces = ((h_a, 0, split), (h_b, split, S))
+                for c, (lo, hi) in enumerate(Z_CHUNKS):
+                    h = bank(h_first_banks[c], f"h0_{c}")
+                    product(h[:, lo:hi], w2_q[t], w2_s[t], z_q[c][:], z_s[c][:])
+                    nc.scalar.copy(win_pos[t][:, lo:hi], h[:, lo:hi])
+                    nc.vector.tensor_scalar(win_neg[t][:, lo:hi], win_pos[t][:, lo:hi], -1.0, None, ALU.mult)
             else:
                 h = bank(t + 1, f"h{t}")
-                product(h, w2_q, w2_s, t, z_q, z_s, 0, S)
-                pieces = ((h, 0, S),)
-            for acc, lo, hi in pieces:
-                nc.scalar.copy(win_pos[t][:, lo:hi], acc[:, lo:hi])
-                nc.scalar.activation(win_neg[t][:, lo:hi], acc[:, lo:hi], ACT.Copy, scale=-1.0)
+                for c, (lo, hi) in enumerate(Z_CHUNKS):
+                    product(h[:, lo:hi], w2_q[t], w2_s[t], z_q[c][:], z_s[c][:])
+                nc.scalar.copy(win_pos[t][:, :S], h[:])
+                nc.scalar.activation(win_neg[t][:, :S], h[:], ACT.Copy, scale=-1.0)
+                h_banks[t] = h
+
+        def gather_e(t, tag):
+            e[t] = keep.tile([P, S], F32, name=f"e{t}", tag=tag)
             nc.vector.tensor_tensor(e[t][:], win_pos[t][:].indirect(n4_t[:]), win_neg[t][:, :S], ALU.add)
-            nc.vector.tensor_tensor(f[t][:], win_neg[t][:].indirect(n3_t[:]), win_pos[t][:, :S], ALU.add)
+
+        def gather_f(t, dst):
+            f[t] = dst
+            for lo, hi in spans(t):
+                nc.vector.tensor_tensor(f[t][:, lo:hi], win_neg[t][:].indirect(entries(n3_t, lo, hi)), win_pos[t][:, lo:hi], ALU.add)
+
+        def add_turned(acc, first, second, lo, hi):
+            for cols in blocks[lo // P : hi // P]:
+                nc.tensor.matmul(acc[:, cols], first[:, cols], ident[:], start=True, stop=False, is_transpose=True)
+                nc.tensor.matmul(acc[:, cols], second[:, cols], ident[:], start=False, stop=True, is_transpose=True)
+
+        def turn_back(acc, src):
+            for cols in blocks:
+                nc.tensor.transpose(acc[:, cols], src[:, cols], ident[:])
+
+        def make_gate(t):
+            gate_t = keep.tile([P, S], F32, name=f"gate_t{t}")
+            for u, (lo, hi) in enumerate(spans(t)):
+                d_t = bank(6 + (t + u) % 2, f"d{t}_{u}")
+                add_turned(d_t, e[t], f[t], lo, hi)
+                nc.scalar.activation(gate_t[:, lo:hi], d_t[:, lo:hi], ACT.Sigmoid, scale=-1.0)
+            gate[t] = bank(gate_bank[t], f"gate{t}")
+            turn_back(gate[t], gate_t)
+
+        def step(t, dst):
+            nc.vector.tensor_tensor(dst, e[t][:], gate[t][:], ALU.mult)
+
+        def store(t, lo, hi):
+            nc.sync.dma_start(out_rows[:, t, lo:hi], res[t][:, lo:hi])
+
         for t in range(PACK):
-            d_t = bank(d_bank[t], f"d{t}")
-            for b in range(S // P):
-                cols = slice(b * P, (b + 1) * P)
-                nc.tensor.matmul(d_t[:, cols], e[t][:, cols], ident[:], start=True, stop=False, is_transpose=True)
-                nc.tensor.matmul(d_t[:, cols], f[t][:, cols], ident[:], start=False, stop=True, is_transpose=True)
-            tau_t = keep.tile([P, S], F32, name=f"tau_t{t}")
-            nc.scalar.activation(tau_t[:], d_t[:], ACT.Tanh, scale=-0.5)
-            back = bank(tau_bank[t], f"tau{t}")
-            for b in range(S // P):
-                cols = slice(b * P, (b + 1) * P)
-                nc.tensor.transpose(back[:, cols], tau_t[:, cols], ident[:])
-            tau.append(back)
-        out_rows = out.rearrange("(p t) s -> p t s", t=PACK)
-        for t in range(PACK):
-            step = keep.tile([P, S], F32, name=f"step{t}")
-            nc.vector.scalar_tensor_tensor(step[:], tau[t][:], 1.0, e[t][:], ALU.add, ALU.mult)
-            res = keep.tile([P, S], F32, name=f"res{t}")
-            nc.vector.scalar_tensor_tensor(res[:], step[:], 0.5, win_pos[t][:, :S], ALU.mult, ALU.add)
-            nc.sync.dma_start(out_rows[:, t, :], res[:])
+            second_product(t)
+        for t in range(last_tile):
+            gather_e(t, f"e{t}")
+            gather_f(t, keep.tile([P, S], F32, name=f"f{t}"))
+            make_gate(t)
+        step0 = keep.tile([P, S], F32, name="step0")
+        step(0, step0[:])
+        gather_e(last_tile, "e0")
+        nc.vector.tensor_tensor(res[0][:], step0[:], win_pos[0][:, :S], ALU.add)
+        store(0, 0, S)
+        gather_f(last_tile, win_pos[0])
+        make_gate(last_tile)
+        steps = (None, win_neg[last_tile][:, :S], win_neg[last_tile][:, S:], f[last_tile][:, :S])
+        step(1, steps[1])
+        nc.gpsimd.tensor_tensor(res[1][:], steps[1], win_pos[1][:, :S], ALU.add)
+        step(2, steps[2])
+        nc.vector.tensor_tensor(res[2][:], steps[2], h_banks[2][:], ALU.add)
+        store(2, 0, S)
+        store(1, 0, S)
+        step(3, steps[3])
+        for lo, hi in spans(last_tile):
+            nc.vector.tensor_tensor(res[3][:, lo:hi], steps[3][:, lo:hi], h_banks[3][:, lo:hi], ALU.add)
+            store(3, lo, hi)

@@ -115,7 +115,9 @@ def tile_picked_tanmix_none_p_kernel(tc, x_words, x_scales, w1, gn, w2, offs, n1
 
         gth = [keep.tile([P, S], F32, name=f"gth{t}") for t in range(PACK)]
         half_gth = win_neg
-        prod = [keep.tile([P, S], F32, name=f"prod{t}") for t in range(PACK)]
+        z_flat = keep.tile([P, PACK * S + HALF], F32, name="z_flat")
+        z_all = z_flat[:, : PACK * S].rearrange("p (t s) -> p t s", t=PACK)
+        prod = [z_flat[:, PACK * S - HALF :] if t == 2 else keep.tile([P, S], F32, name=f"prod{t}")[:] for t in range(PACK)]
         for t in range(PACK):
             th = win_pos[t]
             if t == 0:
@@ -132,8 +134,8 @@ def tile_picked_tanmix_none_p_kernel(tc, x_words, x_scales, w1, gn, w2, offs, n1
                     product(y[:, lo:hi], w1_q[:, t * P : (t + 1) * P], w1_s[:, t * P : (t + 1) * P], xw_g[hf][:], xs_g[:, lo:hi])
                 nc.scalar.activation(th[:, :S], y[:], ACT.Tanh)
                 nc.scalar.activation(gth[t][:], th[:, :S], ACT.Copy, scale=gain[:, t : t + 1])
-            nc.vector.tensor_tensor(prod[t][:], th[:].indirect(n1_t[:]), gth[t][:], ALU.mult)
-        for t in range(PACK):
+            nc.vector.tensor_tensor(prod[t], th[:].indirect(n1_t[:]), gth[t][:], ALU.mult)
+        for t in (0, 1, 3, 2):
             nc.scalar.activation(half_gth[t][:, :S], win_pos[t][:, :S], ACT.Copy, scale=gain_neg_half[:, t : t + 1])
         deal(nc.scalar.copy, w2_bf, w2_raw[1], 64, 128, 0)
 
@@ -143,22 +145,21 @@ def tile_picked_tanmix_none_p_kernel(tc, x_words, x_scales, w1, gn, w2, offs, n1
         z_q = [keep.tile([P, hi - lo], U32, name=f"z_q{c}", align_bytes=64) for c, (lo, hi) in enumerate(Z_CHUNKS)]
         z_s = [keep.tile([P, hi - lo], U8, name=f"z_s{c}", align_bytes=64) for c, (lo, hi) in enumerate(Z_CHUNKS)]
         last_tile = PACK - 1
-        z_bf = [keep.tile([P, hi - lo, PACK], BF16, name=f"z_bf{c}", tag=f"z_bf{c}", align_bytes=64) for c, (lo, hi) in enumerate(Z_CHUNKS)]
-        z_all = keep.tile([P, PACK, S], F32, name="z_all")
-        for t in range(PACK):
-            for lo, hi in ((0, S),) if t < last_tile else ((0, HALF), (HALF, S)):
-                nc.vector.tensor_tensor(z_all[:, t, lo:hi], half_gth[t][:].indirect(entries(n2_t, lo, hi)), prod[t][:, lo:hi], ALU.add)
+        z_bf = {}
+        for t, lo, hi in ((0, 0, S), (1, 0, S), (3, 0, HALF), (2, 0, HALF), (3, HALF, S), (2, HALF, S)):
+            nc.vector.tensor_tensor(z_flat[:, t * S + lo : t * S + hi], half_gth[t][:].indirect(entries(n2_t, lo, hi)), prod[t][:, lo:hi], ALU.add)
         nc.vector.quantize_mx(w2_q0[:].bitcast(FP8X4), w2_s_all[:, :P], w2_flat[:, : PACK * P])
 
         def interleave(c, copy):
             lo, hi = Z_CHUNKS[c]
+            z_bf[c] = keep.tile([P, hi - lo, PACK], BF16, name=f"z_bf{c}", tag="z_bf1" if c == 1 else "z_bf2", align_bytes=64)
             copy(z_bf[c][:].rearrange("p (s i) t -> p s t i", i=PACK), z_all[:, :, lo:hi].rearrange("p t (s i) -> p s t i", i=PACK))
 
         def quantise_z(c):
             nc.vector.quantize_mx(z_q[c][:].bitcast(FP8X4), z_s[c][:], z_bf[c][:].rearrange("p s t -> p (s t)"))
 
         interleave(0, nc.scalar.copy)
-        interleave(1, nc.vector.tensor_copy)
+        interleave(1, nc.scalar.copy)
         quantise_z(0)
         interleave(2, nc.vector.tensor_copy)
         quantise_z(1)
@@ -173,7 +174,6 @@ def tile_picked_tanmix_none_p_kernel(tc, x_words, x_scales, w1, gn, w2, offs, n1
         blocks = [slice(u * P, (u + 1) * P) for u in range(S // P)]
         res = [keep.tile([P, S], F32, name=f"res{t}") for t in range(PACK)]
         h_first_banks = (0, 1, 5)
-        gate_bank = (0, 1, 5, 2)
         h_banks, e, f, gate = {}, {}, {}, {}
 
         def spans(t):
@@ -185,7 +185,10 @@ def tile_picked_tanmix_none_p_kernel(tc, x_words, x_scales, w1, gn, w2, offs, n1
                     h = bank(h_first_banks[c], f"h0_{c}")
                     product(h[:, lo:hi], w2_q[t], w2_s[t], z_q[c][:], z_s[c][:])
                     nc.scalar.copy(win_pos[t][:, lo:hi], h[:, lo:hi])
-                    nc.vector.tensor_scalar(win_neg[t][:, lo:hi], win_pos[t][:, lo:hi], -1.0, None, ALU.mult)
+                    if c == 1:
+                        nc.vector.tensor_scalar(win_neg[t][:, :hi], win_pos[t][:, :hi], -1.0, None, ALU.mult)
+                    if c == 2:
+                        nc.scalar.activation(win_neg[t][:, lo:hi], h[:, lo:hi], ACT.Copy, scale=-1.0)
             else:
                 h = bank(t + 1, f"h{t}")
                 for c, (lo, hi) in enumerate(Z_CHUNKS):
@@ -194,60 +197,56 @@ def tile_picked_tanmix_none_p_kernel(tc, x_words, x_scales, w1, gn, w2, offs, n1
                 nc.scalar.activation(win_neg[t][:, :S], h[:], ACT.Copy, scale=-1.0)
                 h_banks[t] = h
 
-        def gather_e(t, tag):
-            e[t] = keep.tile([P, S], F32, name=f"e{t}", tag=tag)
-            nc.vector.tensor_tensor(e[t][:], win_pos[t][:].indirect(n4_t[:]), win_neg[t][:, :S], ALU.add)
+        def gather_e(t, lo, hi, tag):
+            e[t, lo] = keep.tile([P, hi - lo], F32, name=f"e{t}_{lo}", tag=tag)
+            nc.vector.tensor_tensor(e[t, lo][:], win_pos[t][:].indirect(entries(n4_t, lo, hi)), win_neg[t][:, lo:hi], ALU.add)
 
-        def gather_f(t, dst):
-            f[t] = dst
-            for lo, hi in spans(t):
-                nc.vector.tensor_tensor(f[t][:, lo:hi], win_neg[t][:].indirect(entries(n3_t, lo, hi)), win_pos[t][:, lo:hi], ALU.add)
+        def gather_f(t):
+            f[t] = keep.tile([P, S], F32, name=f"f{t}")
+            nc.vector.tensor_tensor(f[t][:], win_neg[t][:].indirect(n3_t[:]), win_pos[t][:, :S], ALU.add)
 
-        def add_turned(acc, first, second, lo, hi):
-            for cols in blocks[lo // P : hi // P]:
-                nc.tensor.matmul(acc[:, cols], first[:, cols], ident[:], start=True, stop=False, is_transpose=True)
-                nc.tensor.matmul(acc[:, cols], second[:, cols], ident[:], start=False, stop=True, is_transpose=True)
+        def make_gate(t, lo, hi, d_bank, gate_bank):
+            width = hi - lo
+            d_t = bank(d_bank, f"d{t}_{lo}")
+            for cols in blocks[: width // P]:
+                nc.tensor.matmul(d_t[:, cols], f[t][:, lo:hi][:, cols], ident[:], start=True, stop=False, is_transpose=True)
+                nc.tensor.matmul(d_t[:, cols], e[t, lo][:, cols], ident[:], start=False, stop=True, is_transpose=True)
+            gate_t = keep.tile([P, width], F32, name=f"gate_t{t}_{lo}")
+            nc.scalar.activation(gate_t[:], d_t[:, :width], ACT.Sigmoid, scale=-1.0)
+            gate[t, lo] = bank(gate_bank, f"gate{t}_{lo}")
+            for cols in blocks[: width // P]:
+                nc.tensor.transpose(gate[t, lo][:, cols], gate_t[:, cols], ident[:])
 
-        def turn_back(acc, src):
-            for cols in blocks:
-                nc.tensor.transpose(acc[:, cols], src[:, cols], ident[:])
-
-        def make_gate(t):
-            gate_t = keep.tile([P, S], F32, name=f"gate_t{t}")
-            for u, (lo, hi) in enumerate(spans(t)):
-                d_t = bank(6 + (t + u) % 2, f"d{t}_{u}")
-                add_turned(d_t, e[t], f[t], lo, hi)
-                nc.scalar.activation(gate_t[:, lo:hi], d_t[:, lo:hi], ACT.Sigmoid, scale=-1.0)
-            gate[t] = bank(gate_bank[t], f"gate{t}")
-            turn_back(gate[t], gate_t)
-
-        def step(t, dst):
-            nc.vector.tensor_tensor(dst, e[t][:], gate[t][:], ALU.mult)
-
-        def store(t, lo, hi):
-            nc.sync.dma_start(out_rows[:, t, lo:hi], res[t][:, lo:hi])
+        def step(t, lo, hi, dst):
+            nc.vector.tensor_tensor(dst, e[t, lo][:], gate[t, lo][:, : hi - lo], ALU.mult)
 
         for t in range(PACK):
             second_product(t)
         for t in range(last_tile):
-            gather_e(t, f"e{t}")
-            gather_f(t, keep.tile([P, S], F32, name=f"f{t}"))
-            make_gate(t)
+            gather_e(t, 0, S, f"e{t}")
+            gather_f(t)
+            make_gate(t, 0, S, 6 + t % 2, (0, 1, 5)[t])
+        gather_f(last_tile)
+        gather_e(last_tile, 0, HALF, "e3")
+        make_gate(last_tile, 0, HALF, 7, 2)
         step0 = keep.tile([P, S], F32, name="step0")
-        step(0, step0[:])
-        gather_e(last_tile, "e0")
-        nc.vector.tensor_tensor(res[0][:], step0[:], win_pos[0][:, :S], ALU.add)
-        store(0, 0, S)
-        gather_f(last_tile, win_pos[0])
-        make_gate(last_tile)
-        steps = (None, win_neg[last_tile][:, :S], win_neg[last_tile][:, S:], f[last_tile][:, :S])
-        step(1, steps[1])
-        nc.gpsimd.tensor_tensor(res[1][:], steps[1], win_pos[1][:, :S], ALU.add)
-        step(2, steps[2])
-        nc.vector.tensor_tensor(res[2][:], steps[2], h_banks[2][:], ALU.add)
-        store(2, 0, S)
-        store(1, 0, S)
-        step(3, steps[3])
+        step(0, 0, S, step0[:])
+        gather_e(last_tile, HALF, S, "e0")
+        make_gate(last_tile, HALF, S, 6, 0)
+
+        res0 = win_neg[last_tile][:, HALF : HALF + S]
+        step1, step2, step3 = win_pos[last_tile][:, :S], win_pos[last_tile][:, S:], f[last_tile]
         for lo, hi in spans(last_tile):
-            nc.vector.tensor_tensor(res[3][:, lo:hi], steps[3][:, lo:hi], h_banks[3][:, lo:hi], ALU.add)
-            store(3, lo, hi)
+            nc.gpsimd.tensor_tensor(res0[:, lo:hi], step0[:, lo:hi], win_pos[0][:, lo:hi], ALU.add)
+            nc.sync.dma_start(out_rows[:, 0, lo:hi], res0[:, lo:hi])
+        step(2, 0, S, step2)
+        step(1, 0, S, step1)
+        nc.vector.tensor_tensor(res[2][:], step2, h_banks[2][:], ALU.add)
+        nc.sync.dma_start(out_rows[:, 2, :], res[2][:])
+        for lo, hi in spans(last_tile):
+            step(last_tile, lo, hi, step3[:, lo:hi])
+        for lo, hi in spans(last_tile):
+            nc.gpsimd.tensor_tensor(res[1][:, lo:hi], step1[:, lo:hi], win_pos[1][:, lo:hi], ALU.add)
+            nc.sync.dma_start(out_rows[:, 1, lo:hi], res[1][:, lo:hi])
+            nc.vector.tensor_tensor(res[3][:, lo:hi], step3[:, lo:hi], h_banks[3][:, lo:hi], ALU.add)
+            nc.sync.dma_start(out_rows[:, 3, lo:hi], res[3][:, lo:hi])

@@ -63,10 +63,6 @@ def tile_picked_tanmix_none_p_kernel(tc, x_words, x_scales, w1, gn, w2, offs, n1
         n4_t = load_list(n4, "n4_t")
         n3_t = load_list(n3, "n3_t")
 
-        warm = keep.tile([P, 2], F32, name="warm")
-        nc.gpsimd.memset(warm[:], 0.0)
-        nc.scalar.activation(warm[:, 1:2], warm[:, 0:1], ACT.Sigmoid)
-
         ident = keep.tile([P, P], F32, name="ident")
         make_identity(nc, ident[:])
         win_pos = [keep.tile([P, 2 * S], F32, name=f"win_pos{t}") for t in range(PACK)]
@@ -93,7 +89,7 @@ def tile_picked_tanmix_none_p_kernel(tc, x_words, x_scales, w1, gn, w2, offs, n1
         nc.vector.quantize_mx(w1_q[:].bitcast(FP8X4), w1_s[:], w1_bf[:].rearrange("p t m j -> p (t m j)"))
 
         gain_neg_half = keep.tile([P, PACK], F32, name="gain_neg_half")
-        nc.gpsimd.tensor_scalar(gain_neg_half[:], gain[:], -0.5, 0.0, ALU.mult, ALU.add)
+        nc.scalar.activation(gain_neg_half[:], gain[:], ACT.Copy, scale=-0.5)
 
         xw_g = [keep.tile([P, HALF], U32, name=f"xw_g{hf}", align_bytes=64) for hf in range(2)]
         for hf in range(2):
@@ -115,9 +111,10 @@ def tile_picked_tanmix_none_p_kernel(tc, x_words, x_scales, w1, gn, w2, offs, n1
 
         gth = [keep.tile([P, S], F32, name=f"gth{t}") for t in range(PACK)]
         half_gth = win_neg
-        z_flat = keep.tile([P, PACK * S + HALF], F32, name="z_flat")
-        z_all = z_flat[:, : PACK * S].rearrange("p (t s) -> p t s", t=PACK)
-        prod = [z_flat[:, PACK * S - HALF :] if t == 2 else keep.tile([P, S], F32, name=f"prod{t}")[:] for t in range(PACK)]
+        z_lo = keep.tile([P, PACK * HALF], F32, name="z_lo")
+        z_hi = keep.tile([P, (PACK + 1) * HALF], F32, name="z_hi")
+        z_half = (z_lo, z_hi)
+        prod = [z_hi[:, (PACK - 1) * HALF :] if t == 2 else keep.tile([P, S], F32, name=f"prod{t}")[:] for t in range(PACK)]
         for t in range(PACK):
             th = win_pos[t]
             if t == 0:
@@ -146,14 +143,17 @@ def tile_picked_tanmix_none_p_kernel(tc, x_words, x_scales, w1, gn, w2, offs, n1
         z_s = [keep.tile([P, hi - lo], U8, name=f"z_s{c}", align_bytes=64) for c, (lo, hi) in enumerate(Z_CHUNKS)]
         last_tile = PACK - 1
         z_bf = {}
-        for t, lo, hi in ((0, 0, S), (1, 0, S), (3, 0, HALF), (2, 0, HALF), (3, HALF, S), (2, HALF, S)):
-            nc.vector.tensor_tensor(z_flat[:, t * S + lo : t * S + hi], half_gth[t][:].indirect(entries(n2_t, lo, hi)), prod[t][:, lo:hi], ALU.add)
+        for t, hf in ((0, 0), (0, 1), (1, 0), (1, 1), (3, 0), (2, 0), (3, 1), (2, 1)):
+            lo, hi = hf * HALF, (hf + 1) * HALF
+            nc.vector.tensor_tensor(z_half[hf][:, t * HALF : (t + 1) * HALF], half_gth[t][:].indirect(entries(n2_t, lo, hi)), prod[t][:, lo:hi], ALU.add)
         nc.vector.quantize_mx(w2_q0[:].bitcast(FP8X4), w2_s_all[:, :P], w2_flat[:, : PACK * P])
 
         def interleave(c, copy):
             lo, hi = Z_CHUNKS[c]
             z_bf[c] = keep.tile([P, hi - lo, PACK], BF16, name=f"z_bf{c}", tag="z_bf1" if c == 1 else "z_bf2", align_bytes=64)
-            copy(z_bf[c][:].rearrange("p (s i) t -> p s t i", i=PACK), z_all[:, :, lo:hi].rearrange("p t (s i) -> p s t i", i=PACK))
+            hf = lo // HALF
+            src = z_half[hf][:, : PACK * HALF].rearrange("p (t s) -> p t s", t=PACK)[:, :, lo - hf * HALF : hi - hf * HALF]
+            copy(z_bf[c][:].rearrange("p (s i) t -> p s t i", i=PACK), src.rearrange("p t (s i) -> p s t i", i=PACK))
 
         def quantise_z(c):
             nc.vector.quantize_mx(z_q[c][:].bitcast(FP8X4), z_s[c][:], z_bf[c][:].rearrange("p s t -> p (s t)"))
@@ -228,14 +228,14 @@ def tile_picked_tanmix_none_p_kernel(tc, x_words, x_scales, w1, gn, w2, offs, n1
             make_gate(t, 0, S, 6 + t % 2, (0, 1, 5)[t])
         gather_f(last_tile)
         gather_e(last_tile, 0, HALF, "e3")
-        make_gate(last_tile, 0, HALF, 7, 2)
+        make_gate(last_tile, 0, HALF, 7, 7)
         step0 = keep.tile([P, S], F32, name="step0")
         step(0, 0, S, step0[:])
         gather_e(last_tile, HALF, S, "e0")
         make_gate(last_tile, HALF, S, 6, 0)
 
-        res0 = win_neg[last_tile][:, HALF : HALF + S]
-        step1, step2, step3 = win_pos[last_tile][:, :S], win_pos[last_tile][:, S:], f[last_tile]
+        res0 = win_pos[last_tile][:, S:]
+        step1, step2, step3 = f[1][:], f[2][:], f[last_tile]
         for lo, hi in spans(last_tile):
             nc.gpsimd.tensor_tensor(res0[:, lo:hi], step0[:, lo:hi], win_pos[0][:, lo:hi], ALU.add)
             nc.sync.dma_start(out_rows[:, 0, lo:hi], res0[:, lo:hi])
@@ -243,10 +243,12 @@ def tile_picked_tanmix_none_p_kernel(tc, x_words, x_scales, w1, gn, w2, offs, n1
         step(1, 0, S, step1)
         nc.vector.tensor_tensor(res[2][:], step2, h_banks[2][:], ALU.add)
         nc.sync.dma_start(out_rows[:, 2, :], res[2][:])
+        step(last_tile, 0, HALF, step3[:, :HALF])
+        nc.gpsimd.tensor_tensor(res[1][:, :HALF], step1[:, :HALF], win_pos[1][:, :HALF], ALU.add)
+        nc.sync.dma_start(out_rows[:, 1, :HALF], res[1][:, :HALF])
+        nc.vector.tensor_tensor(res[1][:, HALF:], step1[:, HALF:], h_banks[1][:, HALF:], ALU.add)
+        nc.sync.dma_start(out_rows[:, 1, HALF:], res[1][:, HALF:])
+        step(last_tile, HALF, S, step3[:, HALF:])
         for lo, hi in spans(last_tile):
-            step(last_tile, lo, hi, step3[:, lo:hi])
-        for lo, hi in spans(last_tile):
-            nc.gpsimd.tensor_tensor(res[1][:, lo:hi], step1[:, lo:hi], win_pos[1][:, lo:hi], ALU.add)
-            nc.sync.dma_start(out_rows[:, 1, lo:hi], res[1][:, lo:hi])
             nc.vector.tensor_tensor(res[3][:, lo:hi], step3[:, lo:hi], h_banks[3][:, lo:hi], ALU.add)
             nc.sync.dma_start(out_rows[:, 3, lo:hi], res[3][:, lo:hi])

from contextlib import ExitStack

import concourse.mybir as mybir
from concourse.masks import make_identity

K, T, S, H, N = 512, 2048, 512, 512, 512
FLOPS = 2 * K * H * S + 2 * H * N * S

F32 = mybir.dt.float32
BF16 = mybir.dt.bfloat16
I32 = mybir.dt.int32
U32 = mybir.dt.uint32
U16 = mybir.dt.uint16
U8 = mybir.dt.uint8
FP8X4 = mybir.dt.float8_e4m3fn_x4
ALU = mybir.AluOpType
ACT = mybir.ActivationFunctionType

P = 128
PACK = 4
LIST_ROWS = 16
HALF = S // 2
Z_CHUNKS = ((0, 256), (256, 384), (384, 512))


def tile_picked_tanmix_none_p_kernel(tc, x_words, x_scales, w1, gn, w2, offs, n1, n2, n3, n4, out):
    nc = tc.nc
    with ExitStack() as ctx:
        lists = ctx.enter_context(tc.tile_pool(name="lists", bufs=1))
        keep = ctx.enter_context(tc.tile_pool(name="keep", bufs=1))
        psum = ctx.enter_context(tc.psum_pool(name="psum", bufs=1))

        def bank(b, name):
            return psum.tile([P, S], F32, name=name, tag=f"bank{b}")

        def entries(lst, lo, hi):
            return lst[:, lo // LIST_ROWS : hi // LIST_ROWS]

        def load_list(src, name):
            lst = lists.tile([P, S // LIST_ROWS], U16, name=name)
            nc.sync.dma_start(lst[:], src)
            return lst

        xs_win = keep.tile([P, T], U8, name="xs_win", tag="xs_win", align_bytes=64)
        nc.vector.memset(xs_win[:].bitcast(I32), 0)
        w1_raw = keep.tile([P, PACK, H], F32, name="w1_raw")
        nc.sync.dma_start(w1_raw[:], w1.rearrange("(p j) c -> p j c", j=PACK))
        offs_t = load_list(offs, "offs_t")
        n1_t = load_list(n1, "n1_t")
        for q in range(4):
            nc.sync.dma_start(xs_win[32 * q : 32 * q + 4, :].bitcast(I32), x_scales[0][4 * q : 4 * q + 4, :].bitcast(I32))
        xw_win = keep.tile([P, T], U32, name="xw_win", align_bytes=64)
        nc.sync.dma_start(xw_win[:].bitcast(I32), x_words[0].rearrange("p n r -> p (n r)").bitcast(I32))
        gain = keep.tile([P, PACK], F32, name="gain")
        nc.sync.dma_start(gain[:], gn.rearrange("(p t) o -> p (t o)", t=PACK))
        w2_rows = w2.rearrange("(p j) c -> p j c", j=PACK)
        w2_raw = []
        for hf in range(2):
            part = keep.tile([P, PACK, N // 2], F32, name=f"w2_raw{hf}")
            nc.sync.dma_start(part[:], w2_rows[:, :, hf * (N // 2) : (hf + 1) * (N // 2)])
            w2_raw.append(part)
        n2_t = load_list(n2, "n2_t")
        n4_t = load_list(n4, "n4_t")
        n3_t = load_list(n3, "n3_t")

        ident = keep.tile([P, P], F32, name="ident")
        make_identity(nc, ident[:])
        win_pos = [keep.tile([P, 2 * S], F32, name=f"win_pos{t}") for t in range(PACK)]
        win_neg = [keep.tile([P, 2 * S], F32, name=f"win_neg{t}") for t in range(PACK)]
        for t in range(PACK):
            nc.vector.memset(win_pos[t][:, S:], 0.0)
            nc.gpsimd.memset(win_neg[t][:, S:], 0.0)


        def deal(copy, grouped, raw, m_lo, m_hi, c_lo):
            n = m_hi - m_lo
            copy(
                grouped[:, :, m_lo:m_hi, :].rearrange("p t m j -> p m j t"),
                raw[:, :, c_lo : c_lo + PACK * n].rearrange("p j (m t) -> p m j t", t=PACK),
            )

        w1_bf = keep.tile([P, PACK, P, PACK], BF16, name="w1_bf", align_bytes=64)
        deal(nc.scalar.copy, w1_bf, w1_raw, 0, 64, 0)
        deal(nc.vector.tensor_copy, w1_bf, w1_raw, 64, 128, 256)
        xs_g = keep.tile([P, S], U8, name="xs_g", align_bytes=64)
        nc.vector.tensor_copy(xs_g[:], xs_win[:].indirect(offs_t[:]))
        w1_q = keep.tile([P, H], U32, name="w1_q", tag="xs_win", align_bytes=64)
        w1_s = keep.tile([P, H], U8, name="w1_s", align_bytes=64)
        nc.vector.quantize_mx(w1_q[:].bitcast(FP8X4), w1_s[:], w1_bf[:].rearrange("p t m j -> p (t m j)"))

        gain_neg_half = keep.tile([P, PACK], F32, name="gain_neg_half")
        nc.scalar.activation(gain_neg_half[:], gain[:], ACT.Copy, scale=-0.5)

        xw_g = [keep.tile([P, HALF], U32, name=f"xw_g{hf}", align_bytes=64) for hf in range(2)]
        for hf in range(2):
            nc.vector.tensor_copy(xw_g[hf][:], xw_win[:].indirect(entries(offs_t, hf * HALF, (hf + 1) * HALF)))

        def product(acc, wq, ws, xq, xs):
            nc.tensor.matmul_mx(
                acc,
                lhsT=wq.bitcast(FP8X4),
                lhsT_scale=ws,
                rhs=xq.bitcast(FP8X4),
                rhs_scale=xs,
                start=True,
                stop=True,
            )

        w2_bf = keep.tile([P, PACK, P, PACK], BF16, name="w2_bf", align_bytes=64)
        deal(nc.vector.tensor_copy, w2_bf, w2_raw[0], 0, 64, 0)

        gth = [keep.tile([P, S], F32, name=f"gth{t}") for t in range(PACK)]
        half_gth = win_neg
        z_lo = keep.tile([P, PACK * HALF], F32, name="z_lo")
        z_hi = keep.tile([P, (PACK + 1) * HALF], F32, name="z_hi")
        z_half = (z_lo, z_hi)
        prod = [z_hi[:, (PACK - 1) * HALF :] if t == 2 else keep.tile([P, S], F32, name=f"prod{t}")[:] for t in range(PACK)]
        for t in range(PACK):
            th = win_pos[t]
            if t == 0:
                for hf in range(2):
                    lo, hi = hf * HALF, (hf + 1) * HALF
                    y = bank(hf, f"y0_{hf}")
                    product(y[:, lo:hi], w1_q[:, t * P : (t + 1) * P], w1_s[:, t * P : (t + 1) * P], xw_g[hf][:], xs_g[:, lo:hi])
                    nc.scalar.activation(th[:, lo:hi], y[:, lo:hi], ACT.Tanh)
                    nc.vector.tensor_scalar(gth[t][:, lo:hi], th[:, lo:hi], gain[:, t : t + 1], None, ALU.mult)
            else:
                y = bank(t + 1, f"y{t}")
                for hf in range(2):
                    lo, hi = hf * HALF, (hf + 1) * HALF
                    product(y[:, lo:hi], w1_q[:, t * P : (t + 1) * P], w1_s[:, t * P : (t + 1) * P], xw_g[hf][:], xs_g[:, lo:hi])
                nc.scalar.activation(th[:, :S], y[:], ACT.Tanh)
                nc.scalar.activation(gth[t][:], th[:, :S], ACT.Copy, scale=gain[:, t : t + 1])
            nc.vector.tensor_tensor(prod[t], th[:].indirect(n1_t[:]), gth[t][:], ALU.mult)
        for t in (0, 1, 3, 2):
            nc.scalar.activation(half_gth[t][:, :S], win_pos[t][:, :S], ACT.Copy, scale=gain_neg_half[:, t : t + 1])
        deal(nc.scalar.copy, w2_bf, w2_raw[1], 64, 128, 0)

        w2_q0 = keep.tile([P, P], U32, name="w2_q0", align_bytes=64)
        w2_s_all = keep.tile([P, N], U8, name="w2_s_all", align_bytes=64)
        w2_flat = w2_bf[:].rearrange("p t m j -> p (t m j)")
        z_q = [keep.tile([P, hi - lo], U32, name=f"z_q{c}", align_bytes=64) for c, (lo, hi) in enumerate(Z_CHUNKS)]
        z_s = [keep.tile([P, hi - lo], U8, name=f"z_s{c}", align_bytes=64) for c, (lo, hi) in enumerate(Z_CHUNKS)]
        last_tile = PACK - 1
        z_bf = {}
        for t, hf in ((0, 0), (0, 1), (1, 0), (1, 1), (3, 0), (2, 0), (3, 1), (2, 1)):
            lo, hi = hf * HALF, (hf + 1) * HALF
            nc.vector.tensor_tensor(z_half[hf][:, t * HALF : (t + 1) * HALF], half_gth[t][:].indirect(entries(n2_t, lo, hi)), prod[t][:, lo:hi], ALU.add)
        nc.vector.quantize_mx(w2_q0[:].bitcast(FP8X4), w2_s_all[:, :P], w2_flat[:, : PACK * P])

        def interleave(c, copy):
            lo, hi = Z_CHUNKS[c]
            z_bf[c] = keep.tile([P, hi - lo, PACK], BF16, name=f"z_bf{c}", tag="z_bf1" if c == 1 else "z_bf2", align_bytes=64)
            hf = lo // HALF
            src = z_half[hf][:, : PACK * HALF].rearrange("p (t s) -> p t s", t=PACK)[:, :, lo - hf * HALF : hi - hf * HALF]
            copy(z_bf[c][:].rearrange("p (s i) t -> p s t i", i=PACK), src.rearrange("p t (s i) -> p s t i", i=PACK))

        def quantise_z(c):
            nc.vector.quantize_mx(z_q[c][:].bitcast(FP8X4), z_s[c][:], z_bf[c][:].rearrange("p s t -> p (s t)"))

        interleave(0, nc.scalar.copy)
        interleave(1, nc.scalar.copy)
        quantise_z(0)
        interleave(2, nc.vector.tensor_copy)
        quantise_z(1)
        quantise_z(2)
        w2_q_rest = keep.tile([P, 3 * P], U32, name="w2_q_rest", tag="z_bf2", align_bytes=64)
        nc.vector.quantize_mx(w2_q_rest[:, :P].bitcast(FP8X4), w2_s_all[:, P : 2 * P], w2_flat[:, PACK * P : 2 * PACK * P])
        nc.vector.quantize_mx(w2_q_rest[:, P:].bitcast(FP8X4), w2_s_all[:, 2 * P :], w2_flat[:, 2 * PACK * P :])
        w2_q = [w2_q0[:]] + [w2_q_rest[:, u * P : (u + 1) * P] for u in range(3)]
        w2_s = [w2_s_all[:, t * P : (t + 1) * P] for t in range(PACK)]

        out_rows = out.rearrange("(p t) s -> p t s", t=PACK)
        blocks = [slice(u * P, (u + 1) * P) for u in range(S // P)]
        res = [keep.tile([P, S], F32, name=f"res{t}") for t in range(PACK)]
        h_first_banks = (0, 1, 5)
        h_banks, e, f, gate = {}, {}, {}, {}

        def spans(t):
            return ((0, S),) if t < last_tile else ((0, HALF), (HALF, S))

        def second_product(t):
            if t == 0:
                for c, (lo, hi) in enumerate(Z_CHUNKS):
                    h = bank(h_first_banks[c], f"h0_{c}")
                    product(h[:, lo:hi], w2_q[t], w2_s[t], z_q[c][:], z_s[c][:])
                    nc.scalar.copy(win_pos[t][:, lo:hi], h[:, lo:hi])
                    if c == 1:
                        nc.vector.tensor_scalar(win_neg[t][:, :hi], win_pos[t][:, :hi], -1.0, None, ALU.mult)
                    if c == 2:
                        nc.scalar.activation(win_neg[t][:, lo:hi], h[:, lo:hi], ACT.Copy, scale=-1.0)
            else:
                h = bank(t + 1, f"h{t}")
                for c, (lo, hi) in enumerate(Z_CHUNKS):
                    product(h[:, lo:hi], w2_q[t], w2_s[t], z_q[c][:], z_s[c][:])
                nc.scalar.copy(win_pos[t][:, :S], h[:])
                nc.scalar.activation(win_neg[t][:, :S], h[:], ACT.Copy, scale=-1.0)
                h_banks[t] = h

        def gather_e(t, lo, hi, tag):
            e[t, lo] = keep.tile([P, hi - lo], F32, name=f"e{t}_{lo}", tag=tag)
            nc.vector.tensor_tensor(e[t, lo][:], win_pos[t][:].indirect(entries(n4_t, lo, hi)), win_neg[t][:, lo:hi], ALU.add)

        def gather_f(t):
            f[t] = keep.tile([P, S], F32, name=f"f{t}")
            nc.vector.tensor_tensor(f[t][:], win_neg[t][:].indirect(n3_t[:]), win_pos[t][:, :S], ALU.add)

        def make_gate(t, lo, hi, d_bank, gate_bank):
            width = hi - lo
            d_t = bank(d_bank, f"d{t}_{lo}")
            for cols in blocks[: width // P]:
                nc.tensor.matmul(d_t[:, cols], f[t][:, lo:hi][:, cols], ident[:], start=True, stop=False, is_transpose=True)
                nc.tensor.matmul(d_t[:, cols], e[t, lo][:, cols], ident[:], start=False, stop=True, is_transpose=True)
            gate_t = keep.tile([P, width], F32, name=f"gate_t{t}_{lo}")
            nc.scalar.activation(gate_t[:], d_t[:, :width], ACT.Sigmoid, scale=-1.0)
            gate[t, lo] = bank(gate_bank, f"gate{t}_{lo}")
            for cols in blocks[: width // P]:
                nc.tensor.transpose(gate[t, lo][:, cols], gate_t[:, cols], ident[:])

        def step(t, lo, hi, dst):
            nc.vector.tensor_tensor(dst, e[t, lo][:], gate[t, lo][:, : hi - lo], ALU.mult)

        for t in range(PACK):
            second_product(t)
        for t in range(last_tile):
            gather_e(t, 0, S, f"e{t}")
            gather_f(t)
            make_gate(t, 0, S, 6 + t % 2, (0, 1, 5)[t])
        gather_f(last_tile)
        gather_e(last_tile, 0, HALF, "e3")
        make_gate(last_tile, 0, HALF, 7, 7)
        step0 = keep.tile([P, S], F32, name="step0")
        step(0, 0, S, step0[:])
        gather_e(last_tile, HALF, S, "e0")
        make_gate(last_tile, HALF, S, 6, 0)

        res0 = win_pos[last_tile][:, S:]
        step1, step2, step3 = f[1][:], f[2][:], f[last_tile]
        for lo, hi in spans(last_tile):
            nc.gpsimd.tensor_tensor(res0[:, lo:hi], step0[:, lo:hi], win_pos[0][:, lo:hi], ALU.add)
            nc.sync.dma_start(out_rows[:, 0, lo:hi], res0[:, lo:hi])
        step(2, 0, S, step2)
        step(1, 0, S, step1)
        nc.vector.tensor_tensor(res[2][:], step2, h_banks[2][:], ALU.add)
        nc.sync.dma_start(out_rows[:, 2, :], res[2][:])
        step(last_tile, 0, HALF, step3[:, :HALF])
        nc.gpsimd.tensor_tensor(res[1][:, :HALF], step1[:, :HALF], win_pos[1][:, :HALF], ALU.add)
        nc.sync.dma_start(out_rows[:, 1, :HALF], res[1][:, :HALF])
        nc.vector.tensor_tensor(res[1][:, HALF:], step1[:, HALF:], h_banks[1][:, HALF:], ALU.add)
        nc.sync.dma_start(out_rows[:, 1, HALF:], res[1][:, HALF:])
        step(last_tile, HALF, S, step3[:, HALF:])
        for lo, hi in spans(last_tile):
            nc.vector.tensor_tensor(res[3][:, lo:hi], step3[:, lo:hi], h_banks[3][:, lo:hi], ALU.add)
            nc.sync.dma_start(out_rows[:, 3, lo:hi], res[3][:, lo:hi])
